import numpy as np, ml_dtypes
CORES = [8,11,14,16,19,22,24,27,30]
N = 9
import mx_ref
NC = 128
BF = ml_dtypes.bfloat16
def cut(t, i, w=512):
    return t[:, w * i:w * i + w]
def pk(c, s, i=0):
    return (np.ascontiguousarray(c[:, 512 * i:512 * i + 512]), mx_ref.live(s[:, 128 * i:128 * i + 128]))
def inputs(rng, e, E):
    def f(*shape):
        v = (rng.standard_normal(shape, dtype=np.float32) * np.exp2(rng.integers(-2, 3, shape[:-1] + (1,)))).astype(BF)
        return mx_ref.spread((v.astype(np.float32) * np.exp2(rng.integers(-E, E + 1, shape[:-2] + (1, 1))).astype(np.float32)).astype(BF), rng, e)
    def packed(k):
        c = np.zeros((N, 128, k * 512), np.uint8); s = np.zeros((N, 128, k * 128), np.uint8)
        for r in range(N):
            for i in range(k):
                a, b = mx_ref.quantize(f(128, 512)); c[r][:, 512 * i:512 * i + 512] = a; s[r][:, 128 * i:128 * i + 128] = mx_ref.plane(b, rng)
        return c, s
    d = {}
    d["wc"], d["ws"] = packed(N)
    d["x"] = f(N, 128, 4 * NC)
    return d
def setup_inputs(rng):
    return inputs(rng, 0, 0)
def setup_inputs_blocks(rng):
    return inputs(rng, 4, 0)
def setup_inputs_wide(rng):
    return inputs(rng, 0, 8)
def reference(wc, ws, x):
    y = np.zeros((N, 128, N * NC), np.float32)
    for r in range(N):
        X = mx_ref.quantize(x[r])
        for j in range(N):
            y[r][:, NC * j:NC * j + NC] = mx_ref.matmul(pk(wc[j], ws[j], r), X)
    return {"y": y}

@@ -1,0 +1,247 @@
+from concourse.bass import DstId, RemoteDMATransfer
+from concourse.mybir import dt
+
+N = 9
+TW = 128
+NSIM = 32
+BANKS = 8
+BANK = 512
+ROWMAX = 4096
+
+SCRATCH = {
+    "wq": ("sbuf", [128, N * TW], "float8_e4m3fn_x4"),
+    "wp": ("sbuf", [128, N * TW], "uint8"),
+    "rq": ("sbuf", [128, N * TW], "float8_e4m3fn_x4"),
+    "rp": ("sbuf", [128, N * TW], "uint8"),
+    "xb": ("sbuf", [128, 4 * TW], "bfloat16"),
+    "xq": ("sbuf", [128, TW], "float8_e4m3fn_x4"),
+    "xp": ("sbuf", [128, TW], "uint8"),
+    "yb": ("sbuf", [128, N * TW], "float32"),
+    "ps": ("psum", [128, BANKS * BANK], "float32"),
+}
+SEMAPHORES = (["ls", "lx", "lc0", "lc1", "lc2", "hs", "hc", "sent", "xr", "sta", "stb"]
+              + ["a%d" % j for j in range(N)] + ["m%d" % k for k in range(N)] + ["c%d" % k for k in range(N)])
+
+DIRECT_MAX = 1
+
+
+def _bits(mask):
+    out, b = [], 0
+    while mask >> b:
+        if (mask >> b) & 1:
+            out.append(b)
+        b += 1
+    return out
+
+
+def _mk(bits):
+    return sum(1 << b for b in bits)
+
+
+def _rounds(items, bits):
+    out, items = [], list(items)
+    while items:
+        m = 1
+        while 2 * m <= min(len(items), len(bits)):
+            m *= 2
+        w = len(bits) // m
+        out.append([(it, bits[i * w:(i + 1) * w]) for i, it in enumerate(items[:m])])
+        items = items[m:]
+    return out
+
+
+def _plan(cores, topo):
+    n = len(cores)
+    chip, die = topo.chip, topo.die
+    chips = sorted({chip(c) for c in cores})
+    on = {ch: [r for r in range(n) if chip(cores[r]) == ch] for ch in chips}
+    free = [c for c in range(NSIM) if c not in cores]
+
+    def linked(a, b):
+        return topo.mates(a, b) or topo.same_plane(a, b)
+
+    def reach(src, ch):
+        return all(topo.may_write(src, cores[r]) for r in on[ch])
+
+    def helpers(s, ch):
+        out = {}
+        for h in free:
+            hc = chip(h)
+            if hc == ch or not topo.may_write(s, h) or not reach(h, ch):
+                continue
+            far = 0 if die(h) == die(s) else 1
+            if hc == chip(s):
+                out[h] = 1 + far
+            elif linked(chip(s), hc) and linked(hc, ch):
+                out[h] = 3 + far
+        return out
+
+    route = {}
+    for s in cores:
+        opts = sorted((sum(1 for c in helpers(s, ch).values() if c <= 2), len(helpers(s, ch)), ch)
+                      for ch in chips if ch != chip(s) and reach(s, ch))
+        for _, _, ch in opts[:DIRECT_MAX]:
+            route[(s, ch)] = s
+    todo = [(s, ch) for s in cores for ch in chips if ch != chip(s) and (s, ch) not in route]
+    used = []
+    while todo:
+        best = None
+        for b in todo:
+            cand = [(c, h) for h, c in helpers(b[0], b[1]).items() if h not in used]
+            for c, h in cand:
+                key = (c, len(cand), b, h)
+                if best is None or key < best:
+                    best = key
+        route[best[2]] = best[3]
+        used.append(best[3])
+        todo.remove(best[2])
+
+    gops = {c: [] for c in range(NSIM)}
+    sent = {c: 0 for c in range(NSIM)}
+    got, eta, loads, piece = {}, {}, {}, {}
+
+    def xfer(src, kind, buf, a, b, dst, d0, bits, sem):
+        got[(dst, sem)] = got.get((dst, sem), 0) + len(bits)
+        sent[src] += len(bits)
+        return (kind, buf, a, b, dst, d0, _mk(bits), sem)
+
+    def fan(src, kind, buf, first, j, groups):
+        calls = []
+        for ranks, bits, cls in groups:
+            for i, rnd in enumerate(_rounds(ranks, bits)):
+                while len(calls) <= i:
+                    calls.append([])
+                for r, bb in rnd:
+                    calls[i].append(xfer(src, kind, buf, (r - first) * TW, (r - first + 1) * TW,
+                                         cores[r], j * TW, bb, "a%d" % j))
+                    eta[(r, j)] = cls + i
+        return [("send", c) for c in calls]
+
+    for j, s in enumerate(cores):
+        home = chip(s)
+        away = [ch for ch in chips if ch != home]
+        relays = sorted((chip(route[(s, ch)]) == home, ch, route[(s, ch)]) for ch in away if route[(s, ch)] != s)
+        direct = [ch for ch in away if route[(s, ch)] == s]
+        peers = [r for r in on[home] if r != j]
+        every = _bits(topo.mask(s, cores[peers[0]]))
+        spans = [(on[ch][0], on[ch][-1] + 1) for _, ch, _ in relays]
+        for lo, hi in sorted((on[ch][0], on[ch][-1] + 1) for ch in direct + [home]):
+            if len(spans) > len(relays) and spans[-1][1] == lo and (hi - spans[-1][0]) * 4 * TW <= ROWMAX:
+                spans[-1] = (spans[-1][0], hi)
+            else:
+                spans.append((lo, hi))
+        loads[s] = spans
+        for i, (lo, hi) in enumerate(spans):
+            for r in range(lo, hi):
+                piece[(s, r)] = i
+        ops = gops[s]
+        ops.append(("wait", "ls", 16))
+        taken, rel = [], []
+        for _, ch, h in relays:
+            bb = [b for b in _bits(topo.mask(s, h)) if b not in taken][:len(every) // len(relays)]
+            taken += bb
+            rel.append((ch, h, bb))
+        if rel:
+            ops.append(("send", [xfer(s, 0, "w", on[ch][0] * TW, (on[ch][-1] + 1) * TW, h, 0, bb, "hs")
+                                 for ch, h, bb in rel]))
+        for ch, h, bb in rel:
+            ops.append(("wait", "lc%d" % piece[(s, on[ch][0])], 16))
+            ops.append(("send", [xfer(s, 1, "w", on[ch][0] * TW, (on[ch][-1] + 1) * TW, h, 0, bb, "hc")]))
+        groups, rest = [], every
+        if direct:
+            far = [r for ch in direct for r in on[ch]]
+            off = _bits(topo.mask(s, cores[far[0]]))
+            rest = [b for b in every if b not in off]
+            groups.append((far, off, 2))
+        groups.append((peers, rest, 1))
+        ops += fan(s, 0, "w", 0, j, groups)
+        for i in sorted({piece[(s, r)] for ranks, _, _ in groups for r in ranks}):
+            ops.append(("wait", "lc%d" % i, 16))
+        ops += fan(s, 1, "w", 0, j, groups)
+        for ch, h, bb in rel:
+            out = _bits(topo.mask(h, cores[on[ch][0]]))
+            cls = 5 if chip(h) == home else 7
+            gops[h].append(("wait", "hs", len(bb)))
+            gops[h] += fan(h, 0, "r", on[ch][0], j, [(on[ch], out, cls)])
+            gops[h].append(("wait", "hc", len(bb)))
+            gops[h] += fan(h, 1, "r", on[ch][0], j, [(on[ch], out, cls)])
+    return {"gops": gops, "sent": sent, "got": got, "eta": eta, "loads": loads, "piece": piece, "on": on}
+
+
+def rank_program(g, core, T, topo):
+    cores = list(T.cores)
+    P = _plan(cores, topo)
+    sem = T.sem
+    rank = T.rank_of(core)
+
+    def view(kind, buf, a, b):
+        if kind:
+            return (T.wq if buf == "w" else T.rq)[:, a:b].bitcast(dt.uint8)
+        return (T.wp if buf == "w" else T.rp)[:, a:b]
+
+    if rank is not None:
+        g.scalar.dma_start(T.wp[:], T.ws[:]).then_inc(sem.ls, 16)
+        for i, (lo, hi) in enumerate(P["loads"][core]):
+            g.sync.dma_start(T.wq[:, lo * TW:hi * TW].bitcast(dt.uint8),
+                             T.wc[:, lo * 4 * TW:hi * 4 * TW]).then_inc(sem["lc%d" % i], 16)
+        g.scalar.dma_start(T.xb[:], T.x[:]).then_inc(sem.lx, 16)
+
+    for op in P["gops"][core]:
+        if op[0] == "wait":
+            g.wait_ge(sem[op[1]], op[2])
+            continue
+        trs = op[1]
+        if len(trs) == 1:
+            kind, buf, a, b, dst, d0, mask, name = trs[0]
+            rid, pid, _ = topo.addr(dst)
+            g.remote_dma(view(kind, "r", d0, d0 + b - a), view(kind, buf, a, b), sem[name], sem.sent, pid, rid, mask)
+        else:
+            lst = []
+            for kind, buf, a, b, dst, d0, mask, name in trs:
+                rid, pid, _ = topo.addr(dst)
+                lst.append(RemoteDMATransfer(dst_ids=[DstId(rid=rid, pnc=pid)], dma_engine_mask=mask,
+                                             remote_sem=sem[name], src=view(kind, buf, a, b),
+                                             dst=view(kind, "r", d0, d0 + b - a)))
+            g.remote_dma_fused(lst, local_sem=sem.sent)
+    if P["sent"][core]:
+        g.wait_ge(sem.sent, P["sent"][core])
+    if rank is None:
+        return
+
+    g.vector.wait_ge(sem.lx, 16)
+    g.vector.quantize_mx(T.xq[:], T.xp[:], T.xb[:]).then_inc(sem.xr, 1)
+
+    order = [rank] + sorted((j for j in range(N) if j != rank), key=lambda j: (P["eta"][(rank, j)], j))
+    g.tensor.wait_ge(sem.xr, 1)
+    for k, j in enumerate(order):
+        if j == rank:
+            g.tensor.wait_ge(sem.ls, 16)
+            g.tensor.wait_ge(sem["lc%d" % P["piece"][(core, rank)]], 16)
+            wq, wp = T.wq, T.wp
+        else:
+            g.tensor.wait_ge(sem["a%d" % j], P["got"][(core, "a%d" % j)])
+            wq, wp = T.rq, T.rp
+        if k >= BANKS:
+            g.tensor.wait_ge(sem["c%d" % (k - BANKS)], 1)
+        bank = T.ps[:, (k % BANKS) * BANK:(k % BANKS) * BANK + TW]
+        g.tensor.matmul_mx(bank, wq[:, j * TW:(j + 1) * TW], wp[:, j * TW:(j + 1) * TW],
+                           T.xq[:], T.xp[:], True, True).then_inc(sem["m%d" % k], 1)
+        g.vector.wait_ge(sem["m%d" % k], 1)
+        g.vector.tensor_copy(T.yb[:, j * TW:(j + 1) * TW], bank).then_inc(sem["c%d" % k], 1)
+
+    mine = P["on"][topo.chip(core)]
+    nh = len(mine)
+    count = {"sta": 0, "stb": 0}
+    for k in range(nh):
+        g.sync.wait_ge(sem["c%d" % k], 1)
+    g.sync.dma_start(T.y[:, mine[0] * TW:(mine[-1] + 1) * TW],
+                     T.yb[:, mine[0] * TW:(mine[-1] + 1) * TW]).then_inc(sem.sta, 16)
+    count["sta"] += 16
+    for k in range(nh, N):
+        j = order[k]
+        q, name = ((g.scalar, "stb"), (g.sync, "sta"))[(k - nh) % 2]
+        q.wait_ge(sem["c%d" % k], 1)
+        q.dma_start(T.y[:, j * TW:(j + 1) * TW], T.yb[:, j * TW:(j + 1) * TW]).then_inc(sem[name], 16)
+        count[name] += 16
+    g.sync.wait_ge(sem.sta, count["sta"])
+    g.scalar.wait_ge(sem.stb, count["stb"])

@@ -19,10 +19,11 @@ SCRATCH = {
     "yb": ("sbuf", [128, N * TW], "float32"),
     "ps": ("psum", [128, BANKS * BANK], "float32"),
 }
-SEMAPHORES = (["ls", "lx", "lc0", "lc1", "lc2", "hs", "hc", "sent", "xr", "sta", "stb"]
+SEMAPHORES = (["ls", "lx", "lc0", "lc1", "lc2", "hs0", "hc0", "hs1", "hc1", "sent", "xr", "sta", "stb"]
               + ["a%d" % j for j in range(N)] + ["m%d" % k for k in range(N)] + ["c%d" % k for k in range(N)])
 
 DIRECT_MAX = 1
+PART = 2
 
 
 def _bits(mask):
@@ -54,11 +55,23 @@ def _plan(cores, topo):
     n = len(cores)
     chip, die = topo.chip, topo.die
     chips = sorted({chip(c) for c in cores})
+    allchips = sorted({chip(c) for c in range(NSIM)})
     on = {ch: [r for r in range(n) if chip(cores[r]) == ch] for ch in chips}
     free = [c for c in range(NSIM) if c not in cores]
 
     def linked(a, b):
         return topo.mates(a, b) or topo.same_plane(a, b)
+
+    def ports(a, b):
+        ca, cb, d = chip(a), chip(b), die(a)
+        if ca == cb:
+            return []
+        if topo.mates(ca, cb):
+            return [("m", ca, cb, d)]
+        if topo.same_plane(ca, cb):
+            return [("o", ca, d), ("i", cb, d)]
+        m = [x for x in allchips if topo.mates(ca, x) and topo.same_plane(x, cb)][0]
+        return [("m", ca, m, d), ("o", m, d), ("i", cb, d)]
 
     def reach(src, ch):
         return all(topo.may_write(src, cores[r]) for r in on[ch])
@@ -76,57 +89,95 @@ def _plan(cores, topo):
                 out[h] = 3 + far
         return out
 
-    route = {}
+    direct = []
     for s in cores:
         opts = sorted((sum(1 for c in helpers(s, ch).values() if c <= 2), len(helpers(s, ch)), ch)
                       for ch in chips if ch != chip(s) and reach(s, ch))
-        for _, _, ch in opts[:DIRECT_MAX]:
-            route[(s, ch)] = s
-    todo = [(s, ch) for s in cores for ch in chips if ch != chip(s) and (s, ch) not in route]
-    used = []
-    while todo:
-        best = None
-        for b in todo:
-            cand = [(c, h) for h, c in helpers(b[0], b[1]).items() if h not in used]
-            for c, h in cand:
-                key = (c, len(cand), b, h)
-                if best is None or key < best:
-                    best = key
-        route[best[2]] = best[3]
-        used.append(best[3])
-        todo.remove(best[2])
+        direct += [(s, ch) for _, _, ch in opts[:DIRECT_MAX]]
+    parts = []
+    for s in cores:
+        for ch in chips:
+            if ch != chip(s) and (s, ch) not in direct:
+                for i in range(0, len(on[ch]), PART):
+                    parts.append((s, ch, on[ch][i:i + PART]))
+    cand = [helpers(s, ch) for s, ch, _ in parts]
+
+    def cost(asg):
+        load, hl, cls = {}, {}, 0
+        for s, ch in direct:
+            for r in on[ch]:
+                for p in ports(s, cores[r]):
+                    load[p] = load.get(p, 0) + 1
+        for (s, ch, rr), h, cd in zip(parts, asg, cand):
+            for p in ports(s, h):
+                load[p] = load.get(p, 0) + len(rr)
+            for r in rr:
+                for p in ports(h, cores[r]):
+                    load[p] = load.get(p, 0) + 1
+            hl[h] = hl.get(h, 0) + len(rr)
+            cls += cd[h] * len(rr)
+        return (sum(max(0, v - PART) for v in hl.values()), sum(v ** 4 for v in load.values()), cls)
+
+    asg = [sorted(cd)[0] for cd in cand]
+    best, better = cost(asg), True
+    while better:
+        better = False
+        for i in range(len(parts)):
+            for h in sorted(cand[i]):
+                t = asg[:i] + [h] + asg[i + 1:]
+                c = cost(t)
+                if c < best:
+                    best, asg, better = c, t, True
+        for i in range(len(parts)):
+            for k in range(i + 1, len(parts)):
+                if asg[k] in cand[i] and asg[i] in cand[k]:
+                    t = list(asg)
+                    t[i], t[k] = t[k], t[i]
+                    c = cost(t)
+                    if c < best:
+                        best, asg, better = c, t, True
 
     gops = {c: [] for c in range(NSIM)}
     sent = {c: 0 for c in range(NSIM)}
     got, eta, loads, piece = {}, {}, {}, {}
+    slots = {c: [] for c in range(NSIM)}
 
     def xfer(src, kind, buf, a, b, dst, d0, bits, sem):
         got[(dst, sem)] = got.get((dst, sem), 0) + len(bits)
         sent[src] += len(bits)
         return (kind, buf, a, b, dst, d0, _mk(bits), sem)
 
-    def fan(src, kind, buf, first, j, groups):
+    def fan(src, kind, buf, groups):
         calls = []
-        for ranks, bits, cls in groups:
-            for i, rnd in enumerate(_rounds(ranks, bits)):
+        for its, bits in groups:
+            for i, rnd in enumerate(_rounds(its, bits)):
                 while len(calls) <= i:
                     calls.append([])
-                for r, bb in rnd:
-                    calls[i].append(xfer(src, kind, buf, (r - first) * TW, (r - first + 1) * TW,
-                                         cores[r], j * TW, bb, "a%d" % j))
-                    eta[(r, j)] = cls + i
-        return [("send", c) for c in calls]
+                for (a, b, dst, d0, name, key, cls), bb in rnd:
+                    calls[i].append(xfer(src, kind, buf, a, b, dst, d0, bb, name))
+                    if key is not None:
+                        eta[key] = cls + i
+        return [("send", c) for c in calls if c]
+
+    def tile(r, first, j, cls):
+        return ((r - first) * TW, (r - first + 1) * TW, cores[r], j * TW, "a%d" % j, (r, j), cls)
 
     for j, s in enumerate(cores):
         home = chip(s)
-        away = [ch for ch in chips if ch != home]
-        relays = sorted((chip(route[(s, ch)]) == home, ch, route[(s, ch)]) for ch in away if route[(s, ch)] != s)
-        direct = [ch for ch in away if route[(s, ch)] == s]
+        mine = [(ch, rr, h) for (s2, ch, rr), h in zip(parts, asg) if s2 == s]
+        rch = sorted({ch for ch, _, _ in mine},
+                     key=lambda ch: (min(chip(h) == home for c2, _, h in mine if c2 == ch), ch))
+        dch = [ch for s2, ch in direct if s2 == s]
         peers = [r for r in on[home] if r != j]
         every = _bits(topo.mask(s, cores[peers[0]]))
-        spans = [(on[ch][0], on[ch][-1] + 1) for _, ch, _ in relays]
-        for lo, hi in sorted((on[ch][0], on[ch][-1] + 1) for ch in direct + [home]):
-            if len(spans) > len(relays) and spans[-1][1] == lo and (hi - spans[-1][0]) * 4 * TW <= ROWMAX:
+        low = every
+        for c in range(NSIM):
+            if chip(c) != home:
+                low = [b for b in low if b in _bits(topo.mask(s, c))]
+        high = [b for b in every if b not in low]
+        spans = [(on[ch][0], on[ch][-1] + 1) for ch in rch]
+        for lo, hi in sorted((on[ch][0], on[ch][-1] + 1) for ch in dch + [home]):
+            if len(spans) > len(rch) and spans[-1][1] == lo and (hi - spans[-1][0]) * 4 * TW <= ROWMAX:
                 spans[-1] = (spans[-1][0], hi)
             else:
                 spans.append((lo, hi))
@@ -134,37 +185,50 @@ def _plan(cores, topo):
         for i, (lo, hi) in enumerate(spans):
             for r in range(lo, hi):
                 piece[(s, r)] = i
+        wide = {}
+        for ch in rch:
+            for c2, rr, h in mine:
+                if c2 != ch:
+                    continue
+                k = len(slots[h])
+                slots[h].append((j, rr, 5 if chip(h) == home else 7))
+                wide.setdefault(len(rr), []).append((ch, h, rr, k))
+
+        def items(w, kind, chs, where):
+            return [(rr[0] * TW, (rr[-1] + 1) * TW, h, k * PART * TW, ("hc%d" if kind else "hs%d") % k, None, 0)
+                    for ch, h, rr, k in wide.get(w, []) if ch in chs and (chip(h) == home) == where]
+
+        far = [tile(r, 0, j, 2) for ch in dch for r in on[ch]]
+        near = [tile(r, 0, j, 1) for r in peers]
+        widths = sorted(wide, reverse=True)
         ops = gops[s]
         ops.append(("wait", "ls", 16))
-        taken, rel = [], []
-        for _, ch, h in relays:
-            bb = [b for b in _bits(topo.mask(s, h)) if b not in taken][:len(every) // len(relays)]
-            taken += bb
-            rel.append((ch, h, bb))
-        if rel:
-            ops.append(("send", [xfer(s, 0, "w", on[ch][0] * TW, (on[ch][-1] + 1) * TW, h, 0, bb, "hs")
-                                 for ch, h, bb in rel]))
-        for ch, h, bb in rel:
+        for w in widths:
+            if w > 1:
+                ops += fan(s, 0, "w", [(items(w, 0, rch, False), low), (items(w, 0, rch, True), high)])
+        ops += fan(s, 0, "w", [(items(1, 0, rch, False) + far, low), (items(1, 0, rch, True) + near, high)])
+        for ch in rch:
             ops.append(("wait", "lc%d" % piece[(s, on[ch][0])], 16))
-            ops.append(("send", [xfer(s, 1, "w", on[ch][0] * TW, (on[ch][-1] + 1) * TW, h, 0, bb, "hc")]))
-        groups, rest = [], every
-        if direct:
-            far = [r for ch in direct for r in on[ch]]
-            off = _bits(topo.mask(s, cores[far[0]]))
-            rest = [b for b in every if b not in off]
-            groups.append((far, off, 2))
-        groups.append((peers, rest, 1))
-        ops += fan(s, 0, "w", 0, j, groups)
-        for i in sorted({piece[(s, r)] for ranks, _, _ in groups for r in ranks}):
+            away = any(items(w, 1, [ch], False) for w in widths)
+            turn = 0
+            for w in widths:
+                here = items(w, 1, [ch], True)
+                if away:
+                    ops += fan(s, 1, "w", [(items(w, 1, [ch], False), low), (here, high)])
+                elif here:
+                    ops += fan(s, 1, "w", [(here, (high, low)[turn % 2])])
+                    turn += 1
+        for i in sorted({piece[(s, r)] for ch in dch + [home] for r in on[ch]}):
             ops.append(("wait", "lc%d" % i, 16))
-        ops += fan(s, 1, "w", 0, j, groups)
-        for ch, h, bb in rel:
-            out = _bits(topo.mask(h, cores[on[ch][0]]))
-            cls = 5 if chip(h) == home else 7
-            gops[h].append(("wait", "hs", len(bb)))
-            gops[h] += fan(h, 0, "r", on[ch][0], j, [(on[ch], out, cls)])
-            gops[h].append(("wait", "hc", len(bb)))
-            gops[h] += fan(h, 1, "r", on[ch][0], j, [(on[ch], out, cls)])
+        ops += fan(s, 1, "w", [(far, low), (near, high)])
+
+    for h in free:
+        for kind in (0, 1):
+            for k, (j, rr, cls) in enumerate(slots[h]):
+                name = ("hc%d" if kind else "hs%d") % k
+                out = _bits(topo.mask(h, cores[rr[0]]))
+                gops[h].append(("wait", name, got[(h, name)]))
+                gops[h] += fan(h, kind, "r", [([tile(r, rr[0] - k * PART, j, cls) for r in rr], out)])
     return {"gops": gops, "sent": sent, "got": got, "eta": eta, "loads": loads, "piece": piece, "on": on}
 
 

from concourse.bass import DstId, RemoteDMATransfer
from concourse.mybir import dt

N = 9
TW = 128
NSIM = 32
BANKS = 8
BANK = 512
ROWMAX = 4096

SCRATCH = {
    "wq": ("sbuf", [128, N * TW], "float8_e4m3fn_x4"),
    "wp": ("sbuf", [128, N * TW], "uint8"),
    "rq": ("sbuf", [128, N * TW], "float8_e4m3fn_x4"),
    "rp": ("sbuf", [128, N * TW], "uint8"),
    "xb": ("sbuf", [128, 4 * TW], "bfloat16"),
    "xq": ("sbuf", [128, TW], "float8_e4m3fn_x4"),
    "xp": ("sbuf", [128, TW], "uint8"),
    "yb": ("sbuf", [128, N * TW], "float32"),
    "ps": ("psum", [128, BANKS * BANK], "float32"),
}
SEMAPHORES = (["ls", "lx", "lc0", "lc1", "lc2", "hs0", "hc0", "hs1", "hc1", "sent", "xr", "sta", "stb"]
              + ["a%d" % j for j in range(N)] + ["m%d" % k for k in range(N)] + ["c%d" % k for k in range(N)])

DIRECT_MAX = 1
PART = 2


def _bits(mask):
    out, b = [], 0
    while mask >> b:
        if (mask >> b) & 1:
            out.append(b)
        b += 1
    return out


def _mk(bits):
    return sum(1 << b for b in bits)


def _rounds(items, bits):
    out, items = [], list(items)
    while items:
        m = 1
        while 2 * m <= min(len(items), len(bits)):
            m *= 2
        w = len(bits) // m
        out.append([(it, bits[i * w:(i + 1) * w]) for i, it in enumerate(items[:m])])
        items = items[m:]
    return out


def _plan(cores, topo):
    n = len(cores)
    chip, die = topo.chip, topo.die
    chips = sorted({chip(c) for c in cores})
    allchips = sorted({chip(c) for c in range(NSIM)})
    on = {ch: [r for r in range(n) if chip(cores[r]) == ch] for ch in chips}
    free = [c for c in range(NSIM) if c not in cores]

    def linked(a, b):
        return topo.mates(a, b) or topo.same_plane(a, b)

    def ports(a, b):
        ca, cb, d = chip(a), chip(b), die(a)
        if ca == cb:
            return []
        if topo.mates(ca, cb):
            return [("m", ca, cb, d)]
        if topo.same_plane(ca, cb):
            return [("o", ca, d), ("i", cb, d)]
        m = [x for x in allchips if topo.mates(ca, x) and topo.same_plane(x, cb)][0]
        return [("m", ca, m, d), ("o", m, d), ("i", cb, d)]

    def reach(src, ch):
        return all(topo.may_write(src, cores[r]) for r in on[ch])

    def helpers(s, ch):
        out = {}
        for h in free:
            hc = chip(h)
            if hc == ch or not topo.may_write(s, h) or not reach(h, ch):
                continue
            far = 0 if die(h) == die(s) else 1
            if hc == chip(s):
                out[h] = 1 + far
            elif linked(chip(s), hc) and linked(hc, ch):
                out[h] = 3 + far
        return out

    direct = []
    for s in cores:
        opts = sorted((sum(1 for c in helpers(s, ch).values() if c <= 2), len(helpers(s, ch)), ch)
                      for ch in chips if ch != chip(s) and reach(s, ch))
        direct += [(s, ch) for _, _, ch in opts[:DIRECT_MAX]]
    parts = []
    for s in cores:
        for ch in chips:
            if ch != chip(s) and (s, ch) not in direct:
                for i in range(0, len(on[ch]), PART):
                    parts.append((s, ch, on[ch][i:i + PART]))
    cand = [helpers(s, ch) for s, ch, _ in parts]

    def cost(asg):
        load, hl, cls = {}, {}, 0
        for s, ch in direct:
            for r in on[ch]:
                for p in ports(s, cores[r]):
                    load[p] = load.get(p, 0) + 1
        for (s, ch, rr), h, cd in zip(parts, asg, cand):
            for p in ports(s, h):
                load[p] = load.get(p, 0) + len(rr)
            for r in rr:
                for p in ports(h, cores[r]):
                    load[p] = load.get(p, 0) + 1
            hl[h] = hl.get(h, 0) + len(rr)
            cls += cd[h] * len(rr)
        return (sum(max(0, v - PART) for v in hl.values()), sum(v ** 4 for v in load.values()), cls)

    asg = [sorted(cd)[0] for cd in cand]
    best, better = cost(asg), True
    while better:
        better = False
        for i in range(len(parts)):
            for h in sorted(cand[i]):
                t = asg[:i] + [h] + asg[i + 1:]
                c = cost(t)
                if c < best:
                    best, asg, better = c, t, True
        for i in range(len(parts)):
            for k in range(i + 1, len(parts)):
                if asg[k] in cand[i] and asg[i] in cand[k]:
                    t = list(asg)
                    t[i], t[k] = t[k], t[i]
                    c = cost(t)
                    if c < best:
                        best, asg, better = c, t, True

    gops = {c: [] for c in range(NSIM)}
    sent = {c: 0 for c in range(NSIM)}
    got, eta, loads, piece = {}, {}, {}, {}
    slots = {c: [] for c in range(NSIM)}

    def xfer(src, kind, buf, a, b, dst, d0, bits, sem):
        got[(dst, sem)] = got.get((dst, sem), 0) + len(bits)
        sent[src] += len(bits)
        return (kind, buf, a, b, dst, d0, _mk(bits), sem)

    def fan(src, kind, buf, groups):
        calls = []
        for its, bits in groups:
            for i, rnd in enumerate(_rounds(its, bits)):
                while len(calls) <= i:
                    calls.append([])
                for (a, b, dst, d0, name, key, cls), bb in rnd:
                    calls[i].append(xfer(src, kind, buf, a, b, dst, d0, bb, name))
                    if key is not None:
                        eta[key] = cls + i
        return [("send", c) for c in calls if c]

    def tile(r, first, j, cls):
        return ((r - first) * TW, (r - first + 1) * TW, cores[r], j * TW, "a%d" % j, (r, j), cls)

    for j, s in enumerate(cores):
        home = chip(s)
        mine = [(ch, rr, h) for (s2, ch, rr), h in zip(parts, asg) if s2 == s]
        rch = sorted({ch for ch, _, _ in mine},
                     key=lambda ch: (min(chip(h) == home for c2, _, h in mine if c2 == ch), ch))
        dch = [ch for s2, ch in direct if s2 == s]
        peers = [r for r in on[home] if r != j]
        every = _bits(topo.mask(s, cores[peers[0]]))
        low = every
        for c in range(NSIM):
            if chip(c) != home:
                low = [b for b in low if b in _bits(topo.mask(s, c))]
        high = [b for b in every if b not in low]
        spans = [(on[ch][0], on[ch][-1] + 1) for ch in rch]
        for lo, hi in sorted((on[ch][0], on[ch][-1] + 1) for ch in dch + [home]):
            if len(spans) > len(rch) and spans[-1][1] == lo and (hi - spans[-1][0]) * 4 * TW <= ROWMAX:
                spans[-1] = (spans[-1][0], hi)
            else:
                spans.append((lo, hi))
        loads[s] = spans
        for i, (lo, hi) in enumerate(spans):
            for r in range(lo, hi):
                piece[(s, r)] = i
        wide = {}
        for ch in rch:
            for c2, rr, h in mine:
                if c2 != ch:
                    continue
                k = len(slots[h])
                slots[h].append((j, rr, 5 if chip(h) == home else 7))
                wide.setdefault(len(rr), []).append((ch, h, rr, k))

        def items(w, kind, chs, where):
            return [(rr[0] * TW, (rr[-1] + 1) * TW, h, k * PART * TW, ("hc%d" if kind else "hs%d") % k, None, 0)
                    for ch, h, rr, k in wide.get(w, []) if ch in chs and (chip(h) == home) == where]

        far = [tile(r, 0, j, 2) for ch in dch for r in on[ch]]
        near = [tile(r, 0, j, 1) for r in peers]
        widths = sorted(wide, reverse=True)
        ops = gops[s]
        ops.append(("wait", "ls", 16))
        for w in widths:
            if w > 1:
                ops += fan(s, 0, "w", [(items(w, 0, rch, False), low), (items(w, 0, rch, True), high)])
        ops += fan(s, 0, "w", [(items(1, 0, rch, False) + far, low), (items(1, 0, rch, True) + near, high)])
        for ch in rch:
            ops.append(("wait", "lc%d" % piece[(s, on[ch][0])], 16))
            away = any(items(w, 1, [ch], False) for w in widths)
            turn = 0
            for w in widths:
                here = items(w, 1, [ch], True)
                if away:
                    ops += fan(s, 1, "w", [(items(w, 1, [ch], False), low), (here, high)])
                elif here:
                    ops += fan(s, 1, "w", [(here, (high, low)[turn % 2])])
                    turn += 1
        for i in sorted({piece[(s, r)] for ch in dch + [home] for r in on[ch]}):
            ops.append(("wait", "lc%d" % i, 16))
        ops += fan(s, 1, "w", [(far, low), (near, high)])

    for h in free:
        for kind in (0, 1):
            for k, (j, rr, cls) in enumerate(slots[h]):
                name = ("hc%d" if kind else "hs%d") % k
                out = _bits(topo.mask(h, cores[rr[0]]))
                gops[h].append(("wait", name, got[(h, name)]))
                gops[h] += fan(h, kind, "r", [([tile(r, rr[0] - k * PART, j, cls) for r in rr], out)])
    return {"gops": gops, "sent": sent, "got": got, "eta": eta, "loads": loads, "piece": piece, "on": on}


def rank_program(g, core, T, topo):
    cores = list(T.cores)
    P = _plan(cores, topo)
    sem = T.sem
    rank = T.rank_of(core)

    def view(kind, buf, a, b):
        if kind:
            return (T.wq if buf == "w" else T.rq)[:, a:b].bitcast(dt.uint8)
        return (T.wp if buf == "w" else T.rp)[:, a:b]

    if rank is not None:
        g.scalar.dma_start(T.wp[:], T.ws[:]).then_inc(sem.ls, 16)
        for i, (lo, hi) in enumerate(P["loads"][core]):
            g.sync.dma_start(T.wq[:, lo * TW:hi * TW].bitcast(dt.uint8),
                             T.wc[:, lo * 4 * TW:hi * 4 * TW]).then_inc(sem["lc%d" % i], 16)
        g.scalar.dma_start(T.xb[:], T.x[:]).then_inc(sem.lx, 16)

    for op in P["gops"][core]:
        if op[0] == "wait":
            g.wait_ge(sem[op[1]], op[2])
            continue
        trs = op[1]
        if len(trs) == 1:
            kind, buf, a, b, dst, d0, mask, name = trs[0]
            rid, pid, _ = topo.addr(dst)
            g.remote_dma(view(kind, "r", d0, d0 + b - a), view(kind, buf, a, b), sem[name], sem.sent, pid, rid, mask)
        else:
            lst = []
            for kind, buf, a, b, dst, d0, mask, name in trs:
                rid, pid, _ = topo.addr(dst)
                lst.append(RemoteDMATransfer(dst_ids=[DstId(rid=rid, pnc=pid)], dma_engine_mask=mask,
                                             remote_sem=sem[name], src=view(kind, buf, a, b),
                                             dst=view(kind, "r", d0, d0 + b - a)))
            g.remote_dma_fused(lst, local_sem=sem.sent)
    if P["sent"][core]:
        g.wait_ge(sem.sent, P["sent"][core])
    if rank is None:
        return

    g.vector.wait_ge(sem.lx, 16)
    g.vector.quantize_mx(T.xq[:], T.xp[:], T.xb[:]).then_inc(sem.xr, 1)

    order = [rank] + sorted((j for j in range(N) if j != rank), key=lambda j: (P["eta"][(rank, j)], j))
    g.tensor.wait_ge(sem.xr, 1)
    for k, j in enumerate(order):
        if j == rank:
            g.tensor.wait_ge(sem.ls, 16)
            g.tensor.wait_ge(sem["lc%d" % P["piece"][(core, rank)]], 16)
            wq, wp = T.wq, T.wp
        else:
            g.tensor.wait_ge(sem["a%d" % j], P["got"][(core, "a%d" % j)])
            wq, wp = T.rq, T.rp
        if k >= BANKS:
            g.tensor.wait_ge(sem["c%d" % (k - BANKS)], 1)
        bank = T.ps[:, (k % BANKS) * BANK:(k % BANKS) * BANK + TW]
        g.tensor.matmul_mx(bank, wq[:, j * TW:(j + 1) * TW], wp[:, j * TW:(j + 1) * TW],
                           T.xq[:], T.xp[:], True, True).then_inc(sem["m%d" % k], 1)
        g.vector.wait_ge(sem["m%d" % k], 1)
        g.vector.tensor_copy(T.yb[:, j * TW:(j + 1) * TW], bank).then_inc(sem["c%d" % k], 1)

    mine = P["on"][topo.chip(core)]
    nh = len(mine)
    count = {"sta": 0, "stb": 0}
    for k in range(nh):
        g.sync.wait_ge(sem["c%d" % k], 1)
    g.sync.dma_start(T.y[:, mine[0] * TW:(mine[-1] + 1) * TW],
                     T.yb[:, mine[0] * TW:(mine[-1] + 1) * TW]).then_inc(sem.sta, 16)
    count["sta"] += 16
    for k in range(nh, N):
        j = order[k]
        q, name = ((g.scalar, "stb"), (g.sync, "sta"))[(k - nh) % 2]
        q.wait_ge(sem["c%d" % k], 1)
        q.dma_start(T.y[:, j * TW:(j + 1) * TW], T.yb[:, j * TW:(j + 1) * TW]).then_inc(sem[name], 16)
        count[name] += 16
    g.sync.wait_ge(sem.sta, count["sta"])
    g.scalar.wait_ge(sem.stb, count["stb"])
